import numpy as np, ml_dtypes
CORES = [25,29,65,69,153,157,193,197]
N = 8
import mx_ref
BF = ml_dtypes.bfloat16
def gcols(t, e):
    v = np.concatenate([t.reshape(8, 16, -1, 4), np.zeros((8, 16, 1, 4), BF)], axis=2)
    return np.ascontiguousarray(np.stack([v[g][:, e[g]] for g in range(8)])).reshape(128, -1)
def tile(rs):
    return np.stack(rs, axis=2).reshape(128, -1).astype(BF)
def pick(q, e):
    c = np.concatenate([q[0].reshape(128, -1, 4), np.zeros((128, 1, 4), np.uint8)], axis=1); s = np.concatenate([q[1], np.ones((16, 1), np.uint8)], axis=1)
    return (np.ascontiguousarray(c[:, e].reshape(128, -1)), np.ascontiguousarray(s[:, e]))
def join(*qs):
    return (np.concatenate([q[0] for q in qs], axis=1), np.concatenate([q[1] for q in qs], axis=1))
def put(q, e, v):
    c, s = q[0].reshape(128, -1, 4).copy(), q[1].copy(); c[:, e] = v[0].reshape(128, -1, 4); s[:, e] = v[1]
    return (c.reshape(128, -1), s)
def pk(c, s):
    return (np.ascontiguousarray(c), mx_ref.live(s))
def emit(q):
    return q[0], q[1]
def packed(v, rng):
    q = [mx_ref.quantize(np.ascontiguousarray(v[r])) for r in range(N)]
    return np.stack([a for a, b in q]), np.stack([mx_ref.plane(b, rng) for a, b in q])
def values_of_codes():
    e, c = np.zeros((128, 128, 4), np.float32), np.zeros((128, 2, 4), np.uint8)
    e[np.arange(128), np.arange(128), 0] = 1
    c[:127, :, 0] = np.arange(256).reshape(2, 128).T[:127]
    return mx_ref.matmul(mx_ref.quantize(e.reshape(128, 512).astype(BF)), (c.reshape(128, 8), np.full((16, 2), 127, np.uint8))).T.reshape(-1).astype(np.float64)
CODE_VALUE, SCALE_VALUE = values_of_codes(), 2.0 ** (np.arange(256) - 127.0)
def decode(q):
    return (CODE_VALUE[q[0]].reshape(16, 8, -1, 4) * SCALE_VALUE[q[1]][:, None, :, None] + 0.0).reshape(128, -1).astype(np.float32)
def f(rng, *shape):
    return mx_ref.flush((rng.standard_normal(shape, dtype=np.float32) * np.exp2(rng.integers(-2, 3, shape[:-1] + (1,)))).astype(BF))
def wide(rng, *shape, cols=0):
    v = rng.standard_normal(shape, dtype=np.float32) * np.exp2(rng.integers(-12, 13, shape)).astype(np.float32)
    if cols: v *= np.repeat(np.exp2(rng.integers(-cols, cols + 1, shape[:-2] + (1, shape[-1] // 4))) * (rng.random(shape[:-2] + (1, shape[-1] // 4)) > 0.0625), 4, axis=-1).astype(np.float32)
    return mx_ref.flush(v.astype(BF))
C, H = 288, 128
MASK = [1, 2, 4]
def big(v):
    v = v.astype(np.float32)
    v[np.abs(v) < np.float32(2.0 ** -16)] = 0
    return v.astype(BF)
def numbers_of(rng):
    return {"x": big(f(rng, N, 128, 4 * C)), "u": np.array(f(rng, N, 128, 512)), "v": np.array(f(rng, N, 128, 512))}
def layers(rng, k=1.0):
    return big(np.clip(rng.standard_normal((N, 128, 2048), dtype=np.float32), -4, 4) * np.float32(k)).reshape(N, 8, 16, 4, 8, 16, 4)
def weights(rng, w):
    c, p = packed(np.ascontiguousarray(w).reshape(N, 128, 2048), rng)
    return {"wc": c, "ws": p}
def setup_inputs(rng):
    return {**numbers_of(rng), **weights(rng, layers(rng))}
def setup_inputs_ties(rng):
    d = numbers_of(rng)
    e = rng.permutation(N)
    x = d["x"].reshape(N, 8, 16, C, 4)
    for r in range(N):
        k = rng.permutation(C) % 3
        if r == e[0]: k = np.zeros(C, int)
        elif r in e[2::2]: k = rng.permutation(3)[np.arange(C) % 3]
        a = x[r][:, :8, :3].copy()
        a[:, :, 2] = 0
        x[r][:, :8] = a[:, :, k]
    x[e[1]] = 0
    u = d["u"].reshape(N, 8, 16, 128, 4)
    for i in range(3): u[:, :, 8:, i::16] = 0
    w = layers(rng)
    w[:, :, :, :, :, :8] = 0
    return {"x": x.reshape(N, 128, 4 * C), "u": u.reshape(N, 128, 512), "v": d["v"], **weights(rng, w)}
def setup_inputs_near(rng):
    d = numbers_of(rng)
    x = d["x"].astype(np.float32).reshape(N, 8, 16, C, 4)
    x[:, :, 0] = 0
    x[:, :, 8:] = 0
    u = d["u"].reshape(N, 128, 128, 4)
    for i in range(3): u[:, :, i::16] = 0
    o = rng.permutation(N) % 4
    for r in range(N):
        k = 1.0 if o[r] == 0 else 2.0 ** -30
        if o[r] < 2:
            x[r, :, 0, :, 0] = rng.integers(0, 2, (8, C)) * 2.0 - 1.0
            s = rng.integers(0, 16, (8, C))
            x[r, :, 8] = ((s[:, :, None] >> np.arange(4)) & 1) * np.exp2(np.arange(4) - 23.0)
            x[r, :, 9, :, 0] = 2.0 ** -10
            x[r, :, 10:12, :, 0] = rng.integers(-1, 2, (8, 2, C)) * 2.0 ** -23
        else:
            x[r, :, 8, :, 0] = rng.integers(8 if o[r] == 2 else -15, 16, (8, C)) * 2.0 ** -29
            x[r, :, 10:14:2, :, 0] = rng.integers(8, 11, (8, 2, C)) * 2.0 ** -32
            x[r, :, 11:15:2, :, 0] = rng.integers(8, 10, (8, 2, C)) * 2.0 ** -32
        for g in rng.permutation(8)[:4]: x[r, g, 0 if o[r] < 2 else 8, rng.integers(C), 0] = 2.0 ** 19 * rng.choice([-1.0, 1.0])
        for h in range(0, 128, 16):
            if o[r] < 2:
                u[r, h, h, 0] = k
                u[r, h + 8, h] = k
                u[r, h + 9, h, 0] = k
                u[r, h + 10, h + 1, 0] = k
                u[r, h + 11, h + 2, 0] = k
            else:
                u[r, h + 8, h, 0] = k
                for i in range(2):
                    u[r, h + 10 + 2 * i, h + 1 + i, 0] = 1.125 * k
                    u[r, h + 11 + 2 * i, h + 1 + i, 0] = -1.25 * k
    w = layers(rng, 0.125)
    for i in [0, 8, 9, 10, 11, 12, 13, 14, 15]:
        w[:, :, i] = 0
        w[:, :, :, :, :, i] = 0
    return {"x": x.reshape(N, 128, 4 * C).astype(BF), "u": u.reshape(N, 128, 512), "v": d["v"], **weights(rng, w)}
def setup_inputs_late(rng):
    d = numbers_of(rng)
    x = d["x"].astype(np.float32).reshape(N, 8, 16, C, 4)
    k = (1 + 2 * rng.integers(0, 64, (N, 8, 8, C, 4))) * 2.0 ** -7
    a = (1.0 + k) * np.exp2(-rng.integers(8, 15, k.shape).astype(np.float64))
    a[:, :, 0, :, 0] = 1.96875
    x[:, :, 8:] = a * rng.choice([-1.0, 1.0], k.shape) * np.exp2(rng.integers(0, 3, (N, 8, 1, C, 1)).astype(np.float64))
    h = rng.permutation(8)
    x[:, h[0], 8:] *= np.float32(0.125)
    x[:, h[0], 8, :, 0] = np.where(rng.integers(0, 2, (N, C)) == 0, 3.0, 0.9375)
    x[:, h[1], 8:] = 0
    x[:, :, 0] = 0
    i = int(rng.integers(0, 2))
    for r in range(N):
        out = (r + i) % 2 == 0
        x[r, :, 0, :, 0] = 0.25 if out else -0.25
        x[r, :, 0, :, 1] = 0.25 if out or (r // 2) % 2 == 0 else -0.25
        if out:
            x[r, ::2, 0, C - 1, 0] = -0.25
            x[r, ::4, 0, C - 1, 1] = -0.25
    u = d["u"].reshape(N, 128, 128, 4)
    u[:, :, 1::16] = 0
    u[:, :, 2::16] = 0
    for g in range(0, 128, 16):
        u[:, g, g + 1, 0] = 1
        u[:, g, g + 2, 1] = 1
    w = layers(rng)
    w[:, :, :, :, h[:2], 8:] = 0
    for p in range(8, 16):
        for b in range(4):
            if p > 8 or b > 0: w[:, h[0], p, b, h[1], p, b] = 1
    return {"x": x.reshape(N, 128, 4 * C).astype(BF), "u": u.reshape(N, 128, 512), "v": d["v"], **weights(rng, w)}
def setup_inputs_ends(rng):
    d = numbers_of(rng)
    u = d["u"].reshape(N, 8, 16, 128, 4)
    for i in range(3): u[:, :, :, i::16] = 0
    x = np.zeros((N, 8, 16, C, 4))
    w = rng.choice([-1.0, 1.0], (N, 128, 2048)) * 2.0 ** -7
    most, o = 1.2890625 * 2.0 ** 29, rng.permutation(N) % 4
    for r in range(N):
        h = rng.permutation(8)
        if o[r] == 0:
            x[r] = -most * (0.9 + 0.1 * rng.random((8, 16, C, 4)))
            x[r, h[:4]] = -most
            u[r, :, :, ::32] = 2.0 ** 30
            u[r, h[:4], :, 16::32] = 2.0 ** 30
            u[r, :, :, 1::16] = -2.0 ** 30
            u[r, :, :, 2::16] = 2.0 ** 30
            w[r] = 2.0 ** -7
        if o[r] == 1:
            x[r] = most * (0.75 + 0.25 * rng.random((8, 16, C, 4))) * rng.choice([-1.0, 1.0], (8, 1, C, 1))
            for g in range(8):
                for i in (0, 1, 3): u[r, h[(g + i) % 8], :, 16 * g] = 2.0 ** 30
                if g % 2:
                    u[r, h[g - 1], :, 16 * g + 1] = 2.0 ** 30
                    u[r, h[g], :, 16 * g + 2] = -2.0 ** 30
        if o[r] == 2:
            x[r] = 2.0 ** -30
            for g in range(8):
                u[r, g, 0, 16 * g, 0] = 2.0 ** -30
                u[r, g, 0, 16 * g + 1, 0] = 2.0 ** -30 if g % 2 else -2.0 ** -30
                u[r, g, 0, 16 * g + 2, 0] = 2.0 ** -30
            w[r] = 0
        if o[r] == 3:
            x[r] = most * rng.choice([-1.0, 1.0], (8, 16, C, 4))
            for i in range(3): u[r, :, :, i::16] = (2.0 ** 30 * rng.choice([-1.0, 1.0], (8, 16, 8, 4))).astype(np.float32).astype(BF)
    d["v"] = (np.where(d["v"] < 0, -1.0, 1.0) * np.where(rng.permutation(N) % 2, 2.0 ** -30, 2.0 ** 30)[:, None, None]).astype(np.float32).astype(BF)
    return {"x": x.astype(np.float32).reshape(N, 128, 4 * C).astype(BF), "u": u.reshape(N, 128, 512), "v": d["v"], **weights(rng, w.astype(np.float32).astype(BF))}
def setup_inputs_spread(rng):
    d = numbers_of(rng)
    d["x"] = big(wide(rng, N, 128, 4 * C, cols=4))
    return {**d, **weights(rng, layers(rng, 0.125))}
def check_inputs(d):
    b = []
    for k in ("x", "u", "v"):
        a = np.abs(d[k].astype(np.float32))
        if not (np.isfinite(a).all() and ((a == 0) | (a >= 2.0 ** -30) & (a <= 2.0 ** 30)).all()): b.append("a value of " + k)
    none, least, most = [emit(mx_ref.quantize(np.full((128, 16), k, np.float32).astype(BF)))[1][0, 0] for k in (0.0, 2.0 ** -30, 2.0 ** 30)]
    n = 0.0
    for r in range(N):
        if ((d["wc"][r] == 0x7F) | (d["wc"][r] == 0xFF)).any(): b.append("wc: a code that is no number")
        s = mx_ref.live(d["ws"][r])
        if ((s != none) & ((s < least) | (s > most))).any(): b.append("ws: a scale out of range")
        n = max(n, float(np.max(np.abs(decode(pk(d["wc"][r], d["ws"][r]))))))
    m, k = float(np.max(np.abs(d["x"].astype(np.float32)))), 1.0 + 20.0 * n
    if not m * k * k * k <= 2.0 ** 30: b.append("x and W together too large")
    return b
def balls(o, out, turn):
    a, b, last = np.zeros_like(o), np.zeros_like(o), np.zeros_like(o)
    np.put_along_axis(last, o, np.zeros_like(o) + np.arange(C), axis=2)
    i, j = np.zeros((N, 8), np.int64), np.ones((N, 8), np.int64)
    n = j + 1
    for c in range(C):
        a[:, :, c] = np.take_along_axis(o, i[:, :, None], axis=2)[:, :, 0]
        b[:, :, c] = np.take_along_axis(o, j[:, :, None], axis=2)[:, :, 0]
        np.put_along_axis(last, a[:, :, c:c + 1], c, axis=2)
        i, j = np.where(out[:, :, c], n % C, np.where(turn[:, :, c], j, i)), np.where(turn[:, :, c], i, j)
        n = n + out[:, :, c]
    return a, b, last
def reference(x, u, v, wc, ws):
    qu = [mx_ref.quantize(u[r]) for r in range(N)]
    lay = [pk(wc[r], ws[r]) for r in range(N)]
    now = [x[r] for r in range(N)]
    for m in MASK:
        q = [mx_ref.quantize(now[r]) for r in range(N)]
        s = np.stack([mx_ref.matmul(qu[r], q[r]) for r in range(N)]) + np.float32(0.0)
        out = s[:, 1::16] > 0
        turn = (s[:, 2::16] > 0) & ~out
        a, b, last = balls(np.argsort(-s[:, ::16], axis=2, kind="stable"), out, turn)
        qz = []
        for r in range(N):
            t = decode(q[r]).astype(BF)
            z = (gcols(t, a[r]).astype(np.float32) + gcols(t, b[r]).astype(np.float32)) * np.float32(0.5)
            qz.append(mx_ref.quantize(z.astype(BF)))
        new = []
        for r in range(N):
            p = join(pick(qz[r ^ m], np.arange(H)), pick(qz[r], np.arange(H, C)))
            w = tile([mx_ref.matmul(pick(lay[r], np.arange(128 * k, 128 * k + 128)), p) * np.float32(0.03125) for k in range(4)])
            new.append((now[r].astype(np.float32) + gcols(w, last[r]).astype(np.float32)).astype(BF))
        now = new
    y, lb = np.zeros((N, 128, C), np.float32), np.zeros((N, 8, C), np.float32)
    oc, osc = np.zeros((N, 128, 4 * C), np.uint8), np.zeros((N, 16, C), np.uint8)
    for r in range(N):
        q = mx_ref.quantize(now[r])
        y[r] = mx_ref.matmul(mx_ref.quantize(v[r]), q)
        lb[r] = last[r]
        oc[r], osc[r] = emit(q)
    return {"y": y, "lb": lb, "oc": oc, "osc": osc}

from concourse.bass import DstId, RemoteDMATransfer
from concourse.mybir import dt, AluOpType, ActivationFunctionType

C, H, K = 288, 128, 18
R = C - H
HALVES = [(H, C), (0, H)]
MASKS = [1, 2, 4]
LIFT, HUGE, TINY, MID = 1664.0, 1e29, 1e-35, 144.0
TILES = [(288, [17, 16, 15, "eq"]), (240, [14, 13, 12, 11]), (176, [10, 9, 8, 7]), (128, [6, 5, 4, 3]), (128, [2, 1, 0])]
ON_SCALAR = [17, 16]
BF, F16, F32, U16, I32, CODE, SC = "bfloat16", "float16", "float32", "uint16", "int32", "float8_e4m3fn_x4", "uint8"


def sb(n, d):
    return ("sbuf", [128, n], d)


SCRATCH = {
    "ps": ("psum", [128, 4096], F32),
    "ub": sb(512, BF), "vb": sb(512, BF), "qu": sb(128, CODE), "su": sb(128, SC), "qu3": sb(384, CODE), "su3": sb(384, SC),
    "qv": sb(128, CODE), "sv": sb(128, SC), "qw": sb(512, CODE), "sw": sb(512, SC),
    "eb": sb(520, BF), "qe": sb(512, CODE), "se": sb(512, SC), "ob": sb(512, BF), "qo": sb(128, CODE), "so": sb(128, SC),
    "uoi": sb(24, I32), "uoff": sb(24, U16), "pi": sb(4, I32), "col": sb(16, F32),
    "i16": sb(C, BF), "g8": sb(128, BF), "iota": sb(304, BF), "ni": sb(C, BF), "cm": sb(C, F32), "r0": sb(C, F32),
    "mm": sb(2 * C, BF), "t0": sb(C, BF), "t1": sb(C, BF), "t2": sb(C, BF), "ones": sb(C, BF),
    "ioff": sb(K, F32), "nioff": sb(K, F32), "dum": sb(K, F32),
    "ms": sb(C, F32), "hh": sb(C, F32), "junk": sb(8 * K * K, BF), "sg": sb(4 * C, BF), "acr": sb(K, F32), "acc": sb(K, F32),
    "ec": sb(C, F32), "yy": sb(K, F32), "rk": sb(K, U16),
    "sa": sb(C, BF), "aa": sb(C, BF), "bb": sb(C, BF), "ph": sb(C, BF), "cd": sb(C, BF), "mx": sb(C, BF), "cs": sb(C, BF),
    "no": sb(2 * C, F16), "eno": sb(2 * C, F16), "nou": sb(2 * K, U16), "ecd": sb(C, BF), "sm": sb(8 * K, F32),
    "sou": sb(K, U16), "ll": sb(640, BF), "lw": sb(C, BF), "lf": sb(C, F32), "el": sb(C, F16), "lu": sb(K, U16),
    "oo": sb(304, BF), "g1": sb(2 * H, BF), "g2": sb(2 * R, BF), "e1": sb(2 * H, F16), "e2": sb(2 * R, F16), "ab2": sb(20, U16),
    "th": sb(4 * C, BF), "tp": sb(4 * C, BF), "gt": sb(4 * C, BF), "vg": sb(4 * C, BF),
    "z1": sb(4 * H, BF), "q1": sb(H, CODE), "s1": sb(H, SC), "z2": sb(4 * R, BF), "q2": sb(R, CODE), "s2": sb(R, SC),
    "vv": sb(4 * C, BF), "yb": sb(C, F32), "rq": sb(C // 2, CODE), "rs": sb(C, SC), "rl": sb(16, U16),
}
for _i, (_w, _ks) in enumerate(TILES):
    SCRATCH.update({"b%d" % _i: sb(4 * _w, BF), "qb%d" % _i: sb(_w, CODE), "sb%d" % _i: sb(_w, SC)})
for _i in range(4):
    SCRATCH.update({"x%d" % _i: sb(4 * C, BF), "qx%d" % _i: sb(C, CODE), "sx%d" % _i: sb(C, SC)})
for _i in range(3):
    SCRATCH.update({"ql%d" % _i: sb(C, CODE), "sl%d" % _i: sb(C, SC), "ao%d" % _i: sb(16, U16), "al%d" % _i: sb(16, U16)})

SEMAPHORES = (["cv", "cs", "ct", "cg", "sent", "ra", "rb"] + ["arq%d" % i for i in range(3)] + ["arl%d" % i for i in range(3)]
              + ["d%d" % i for i in range(16)])


def bits(engines):
    return sum(1 << e for e in engines)


def route(T, topo, rank, m):
    src, dst = T.cores[rank], T.cores[rank ^ m]
    if topo.may_write(src, dst):
        return src, dst, []
    able = [c for c in topo.cores_of(src) if T.rank_of(c) is None and topo.may_write(c, dst)]
    near = [c for c in able if topo.die(c) == topo.die(src)]
    return src, dst, near[:2]


def arrivals(T, topo, rank, m):
    src, dst, via = route(T, topo, rank, m)
    if not via:
        n = len(topo.engines(src, dst))
        return 2 * n, n
    a, b = len(topo.engines(via[0], dst)), len(topo.engines(via[1], dst))
    return 2 * a + b, b


def hand_on(g, core, T, topo):
    for r, m in enumerate(MASKS):
        for rank in range(len(T.cores)):
            src, dst, via = route(T, topo, rank, m)
            if core not in via:
                continue
            j = via.index(core)
            rid, pid = topo.addr(dst, core)
            e = topo.engines(core, dst)
            n = len(topo.engines(src, core))
            g.wait_ge(T.sem.ra, n // 2)
            g.remote_dma(T["ql%d" % r][:, C // 2 * j:C // 2 * (j + 1)].bitcast(dt.uint8), T.rq[:].bitcast(dt.uint8),
                         T.sem["arq%d" % r], T.sem.sent, pid, rid, bits(e))
            g.wait_ge(T.sem.rb, n)
            if j == 0:
                g.remote_dma(T["sl%d" % r][:], T.rs[:], T.sem["arq%d" % r], T.sem.sent, pid, rid, bits(e))
            else:
                g.remote_dma(T["al%d" % r][:], T.rl[:], T.sem["arl%d" % r], T.sem.sent, pid, rid, bits(e))
            g.wait_ge(T.sem.sent, 2 * len(e))


def rank_program(g, core, T, topo):
    rank = T.rank_of(core)
    if rank is None:
        hand_on(g, core, T, topo)
        return
    A, F = AluOpType, ActivationFunctionType
    Q = {"v": g.vector, "s": g.scalar, "t": g.tensor, "g": g, "y": g.sync}
    count = {"cv": 0, "cs": 0, "ct": 0, "cg": 0}
    known = {q: {} for q in Q}
    log = {}
    total = {"sent": 0}
    free = ["d%d" % i for i in range(16)]

    def w(name, a=0, b=None, s=1):
        if b is None:
            b = T[name].shape[1]
        ap = T[name][:, a:b] if s == 1 else T[name][:, a:b:s]
        return (ap, [(name, a, b, s)])

    def ps(bank, n):
        return (T.ps[:, 512 * bank:512 * bank + n], [("ps%d" % bank, 0, 512, 1)])

    def ind(win, off):
        return (win[0].indirect(off[0]), win[1] + off[1])

    def u8(v):
        return (v[0].bitcast(dt.uint8), v[1])

    def meets(x, y):
        if x[1] <= y[0] or y[1] <= x[0]:
            return False
        return x[2] != y[2] or x[2] == 1 or (x[0] - y[0]) % x[2] == 0

    def wait(q, ev, clock):
        if known[q].get(ev[0], 0) >= ev[1]:
            return
        Q[q].wait_ge(T.sem[ev[0]], ev[1])
        known[q][ev[0]] = ev[1]
        for s, n in clock.items():
            known[q][s] = max(known[q].get(s, 0), n)

    def before(q, outs, ins):
        need = {}
        for vs, writes in ((ins, False), (outs, True)):
            for v in vs:
                for name, a, b, s in v[1]:
                    for lo, hi, st, wr, q0, ev, clock in log.get(name, []):
                        if not meets((a, b, s), (lo, hi, st)) or (q0 == q and q == "t"):
                            continue
                        if wr or writes or (name.startswith("ps") and q0 != q):
                            if need.get(ev[0], (0, None))[0] < ev[1]:
                                need[ev[0]] = (ev[1], clock)
        for s, (n, clock) in sorted(need.items(), key=lambda kv: -sum(kv[1][1].values())):
            wait(q, (s, n), clock)

    def note(q, outs, ins, ev, clock):
        for vs, writes in ((ins, False), (outs, True)):
            for v in vs:
                for name, a, b, s in v[1]:
                    old = log.get(name, [])
                    if writes:
                        old = [e for e in old if not (a <= e[0] and e[1] <= b and (s == 1 or (s == e[2] and (a - e[0]) % s == 0)))]
                    log[name] = old + [(a, b, s, writes, q, ev, clock)]

    def op(q, outs, ins, call):
        before(q, outs, ins)
        s = "c" + q
        count[s] += 1
        call().then_inc(T.sem[s], 1)
        total[s] = count[s]
        note(q, outs, ins, (s, count[s]), dict(known[q]))

    def dma(q, out, in_):
        before(q, [out], [in_])
        s = free.pop(0)
        Q[q].dma_start(out[0], in_[0]).then_inc(T.sem[s], 16)
        total[s] = 16
        note("dma", [out], [in_], (s, 16), dict(known[q]))

    def num(x):
        return x[0] if isinstance(x, tuple) else x

    def views(*xs):
        return [x for x in xs if isinstance(x, tuple)]

    def ts(out, in0, s1, op0, s2=None, op1=None):
        if op1 is None:
            op("v", [out], views(in0, s1), lambda: g.vector.tensor_scalar(out[0], in0[0], num(s1), None, op0))
        else:
            op("v", [out], views(in0, s1, s2), lambda: g.vector.tensor_scalar(out[0], in0[0], num(s1), num(s2), op0, op1))

    def tt(out, in0, in1, o):
        op("v", [out], [in0, in1], lambda: g.vector.tensor_tensor(out[0], in0[0], in1[0], o))

    def cp(out, in_):
        op("v", [out], [in_], lambda: g.vector.tensor_copy(out[0], in_[0]))

    def scatter(win, off, in_):
        op("v", [win], [off, in_], lambda: g.vector.tensor_copy(win[0].indirect(off[0]), in_[0]))

    def scan(out, d0, d1, init, op0, op1):
        op("v", [out], [d0, d1], lambda: g.vector.tensor_tensor_scan(out[0], d0[0], d1[0], init, op0, op1))

    def fill(out, x):
        op("v", [out], [], lambda: g.vector.memset(out[0], x))

    def quant(q, s, t):
        op("v", [q, s], [t], lambda: g.vector.quantize_mx(q[0], s[0], t[0]))

    def act(out, in_, f=F.Copy, bias=None, scale=None, acc=None):
        kw = {}
        if bias is not None:
            kw["bias"] = num(bias)
        if scale is not None:
            kw["scale"] = num(scale)
        if acc is not None:
            kw["accum_out"] = acc[0]
        op("s", views(out, acc), views(in_, bias, scale), lambda: g.scalar.activation(out[0], in_[0], f, **kw))

    def mm(out, lq, ls, rq, rs, start=True, stop=True):
        op("t", [out], [lq, ls, rq, rs], lambda: g.tensor.matmul_mx(out[0], lq[0], ls[0], rq[0], rs[0], start, stop))

    def iota(out, pattern, cm=0, base=0, whole=False):
        if whole:
            op("g", [out], [], lambda: g.iota(out[0], pattern, base, cm))
        else:
            op("g", [out], [], lambda: g.iota(out[0], pattern, base, cm, allow_small_or_imprecise_dtypes=True))

    def to_list(e, src, n):
        scan(w(e, 0, n), w("mm", 0, n), src, 0.0, A.add, A.max)
        return w(e, 15, n, 16)

    def ext(name):
        return (T[name][:], [])

    def plane(name, b, lo=0, hi=C):
        return w(name, C * b + lo, C * b + hi)

    def part(q, s, k):
        return w(q, 128 * k, 128 * k + 128), w(s, 128 * k, 128 * k + 128)

    PCOL, ICOL, GCOL, I1COL, NICOL, E15, DOWN, DOWN1, DOWNC, UPW, UPD, UPX = [w("col", j, j + 1) for j in range(12)]

    def pick_u(r):
        off = w("uoff", 8 * r, 8 * r + 8)
        out, win = w("qu3", 128 * r, 128 * r + 128), w("qu")
        op("v", [out], [win, off],
           lambda: g.vector.tensor_copy(out[0].bitcast(dt.uint32), win[0].bitcast(dt.uint32).indirect(off[0])))
        act(w("su3", 128 * r, 128 * r + 128), ind(w("su"), off))

    def send_state(r):
        src, dst, via = route(T, topo, rank, MASKS[r])
        before("g", [], [w("qx%d" % r), w("sx%d" % r)])
        q, s = T["qx%d" % r], T["sx%d" % r]
        if not via:
            rid, pid = topo.addr(dst, core)
            e = topo.engines(core, dst)
            arr = T.sem["arq%d" % r]
            g.remote_dma(T["ql%d" % r][:].bitcast(dt.uint8), q[:].bitcast(dt.uint8), arr, T.sem.sent, pid, rid, bits(e))
            g.remote_dma(T["sl%d" % r][:], s[:], arr, T.sem.sent, pid, rid, bits(e))
        else:
            e = topo.engines(core, via[0])
            halves = [e[:len(e) // 2], e[len(e) // 2:]]
            moves = []
            for j in range(2):
                rid, pid = topo.addr(via[j], core)
                moves.append(RemoteDMATransfer(dst_ids=[DstId(rid=rid, pnc=pid)], dma_engine_mask=bits(halves[j]), remote_sem=T.sem.ra,
                                               src=q[:, C // 2 * j:C // 2 * (j + 1)].bitcast(dt.uint8), dst=T.rq[:].bitcast(dt.uint8)))
            g.remote_dma_fused(moves, local_sem=T.sem.sent)
            rid, pid = topo.addr(via[0], core)
            g.remote_dma(T.rs[:], s[:], T.sem.rb, T.sem.sent, pid, rid, bits(e))
        total["sent"] += 2 * len(e)
        nq, nl = arrivals(T, topo, rank ^ MASKS[r], MASKS[r])
        total["arq%d" % r], total["arl%d" % r] = nq, nl
        note("far", [w("ql%d" % r), w("sl%d" % r)], [], ("arq%d" % r, nq), {})
        note("far", [w("al%d" % r)], [], ("arl%d" % r, nl), {})

    def send_lists(r):
        src, dst, via = route(T, topo, rank, MASKS[r])
        before("g", [], [w("ao%d" % r)])
        to, land, sem = (via[1], T.rl, T.sem.rb) if via else (dst, T["al%d" % r], T.sem["arl%d" % r])
        rid, pid = topo.addr(to, core)
        e = topo.engines(core, to)
        g.remote_dma(land[:], T["ao%d" % r][:], sem, T.sem.sent, pid, rid, bits(e))
        total["sent"] += len(e)

    def fresh_places():
        iota(w("ll", 0, C), [[1, C]], base=-int(MID))
        iota(w("ll", C, C + 1), [[0, 1]], base=-int(MID))

    dma("s", w("ub"), ext("u"))
    dma("y", w("x0"), ext("x"))
    dma("y", u8(w("qw")), ext("wc"))
    dma("y", w("sw"), ext("ws"))
    dma("y", w("vb"), ext("v"))
    fill(w("ones"), 1.0)
    fill(w("eb"), 0.0)
    iota(w("pi", 0, 1), [[0, 1]], 1, whole=True)
    iota(w("i16"), [[0, K], [1, 16]])
    iota(w("uoi"), [[1, 3], [16, 8]], whole=True)
    iota(w("g8"), [[16, 8], [0, 16]])
    one, out = w("ones", 0, 128), w("eb", 3, 515, 4)
    op("g", [out], [one], lambda: g.affine_select(out[0], one[0], [[-1, 128]], A.is_equal, 0.0, 0, 1))
    ts(w("pi", 1, 2), w("pi", 0, 1), 15, A.bitwise_and)
    ts(w("pi", 2, 3), w("pi", 0, 1), 112, A.bitwise_and)
    lows = [min(16 * k + 16 for k in ks if k != "eq") if len(ks) == 4 else 0 for wd, ks in TILES]
    fill(w("no", 0, 1), 2.0)
    cp(w("col", 0, 3), w("pi", 0, 3))
    fill(w("no", C, C + 1), 0.0)
    for v in (w("b4", 0, 256), w("b4", 256, 512), w("b3", 256, 512)):
        act(v, w("ones", 0, 256), scale=0.0)
    for i in range(3):
        iota(w("b%d" % i, 4 * lows[i]), [[0, 4 * (TILES[i][0] - lows[i])]])
    for v, x in ((w("acc", 0, 1), 0), (w("ph", 0, 1), -320), (w("aa", C - 1, C), 320)):
        iota(v, [[0, 1]], base=x)
    iota(w("ioff"), [[16, K]])
    iota(w("iota", 0, C), [[1, C]], base=-int(MID))
    act(NICOL, ICOL, scale=-1.0)
    act(I1COL, ICOL, F.Identity, bias=1.0)
    act(w("r0"), w("i16"), F.Identity, bias=-HUGE, scale=2.0 * HUGE)
    act(w("t2"), w("i16"), F.Abs, bias=NICOL)
    act(E15, ICOL, F.Relu, bias=-14.0)
    act(w("cm"), w("t2"), F.Identity, bias=HUGE, scale=-2.0 * HUGE)
    ts(w("t0"), w("i16"), ICOL, A.is_equal, 8192.0, A.mult)
    cp(w("uoff"), w("uoi"))
    ts(w("t1"), w("i16"), I1COL, A.is_equal, LIFT, A.mult)
    ts(w("ob", 0, 512, 4), w("g8"), GCOL, A.is_equal)
    tt(w("mm", 0, C), w("t1"), w("t0"), A.subtract)
    quant(w("qu"), w("su"), w("ub"))
    pick_u(0)
    for t in range(1, 4):
        act(w("ob", t, 512, 4), w("ob", 0, 512, 4))

    def late_constants():
        for v, a, b in ((DOWN1, -1, -1.0), (DOWN, -1, 0.0), (DOWNC, -1, MID), (UPW, 3, 640.0), (UPD, 1, 640.0), (UPX, -1, -1300.0)):
            act(v, E15, F.Identity, bias=a * LIFT + b, scale=-a * LIFT)
        act(w("mm", C, 2 * C), w("mm", 0, C))
        act(w("ioff"), w("ioff"), F.Identity, bias=ICOL)
        act(w("ni"), w("iota", 0, C), scale=-1.0 / 256)
        act(w("dum"), w("ioff"), F.Identity, bias=UPD, scale=2.0)
        act(w("nioff"), w("ioff"), F.Identity, bias=MID / 256, scale=-1.0 / 256)

    for r in range(3):
        X, XN = "x%d" % r, "x%d" % (r + 1)
        qx, sx = w("qx%d" % r), w("sx%d" % r)
        far = bool(route(T, topo, rank ^ MASKS[r], MASKS[r])[2])
        for j, (a, b) in enumerate(HALVES):
            quant(w("qx%d" % r, a, b), w("sx%d" % r, a, b), w(X, 4 * a, 4 * b))
            mm(ps(4 + j, b - a), *part("qu3", "su3", 0), w("qx%d" % r, a, b), w("sx%d" % r, a, b))
        if r > 0:
            mm(ps(1, C), *part("qu3", "su3", 1), qx, sx)
            act(w("sa"), ps(1, C), F.Sign, bias=-TINY)
        mm(ps(0, C), *part("qu3", "su3", 0), qx, sx)
        mm(ps(3, C), *part("qu3", "su3", 0), qx, sx)
        send_state(r)
        fresh_places()
        if r == 0:
            pick_u(1)
            pick_u(2)
        if r == 1:
            quant(w("qv"), w("sv"), w("vb"))
        if r == 0:
            mm(ps(1, C), *part("qu3", "su3", 1), qx, sx)
        mm(ps(2, C), *part("qu3", "su3", 2), qx, sx)

        def unpack(q, s):
            for b in range(4):
                mm(ps(4 + b, C), *part("qe", "se", b), q, s)

        for j, (a, b) in enumerate(HALVES):
            tt(w("ms", a, b), ps(4 + j, b - a), w("cm", a, b), A.min)
        if r == 0:
            quant(w("qo"), w("so"), w("ob"))
        else:
            unpack(qx, sx)
        for a, b in HALVES:
            scan(w("hh", a, b), w("r0", a, b), w("ms", a, b), -HUGE, A.min, A.max)
        at = [0]

        def close(i):
            wd = TILES[i][0]
            quant(w("qb%d" % i), w("sb%d" % i), w("b%d" % i))
            mm(ps(3, wd), w("qo"), w("so"), w("qb%d" % i), w("sb%d" % i), i == 0, i == len(TILES) - 1)

        for j, k in enumerate(ON_SCALAR):
            n = 16 * k + 16
            act(plane("sg", j, 0, n), ps(3, n), F.Sign, bias=w("hh", n - 1, n), scale=-1.0)
        for j, k in enumerate(ON_SCALAR):
            t = TILES[0][1].index(k)
            act(w("b0", t, 64 * k, 4), plane("sg", j, 0, 16 * k), F.Relu, acc=w("acr", k, k + 1))
            act(w("b0", 64 * k + t, 64 * k + 64, 4), plane("sg", j, 16 * k, 16 * k + 16), F.Relu)
        pending = []
        for i, (wd, ks) in enumerate(TILES):
            for t, k in enumerate(ks):
                if k in ON_SCALAR:
                    continue
                if k == "eq":
                    tt(w("b%d" % i, t, 4 * C, 4), ps(0, C), w("hh"), A.is_equal)
                else:
                    n = 16 * k + 16
                    ts(w("b%d" % i, t, 4 * n, 4), ps(0, n), w("hh", n - 1, n), A.is_lt)
                    if k > 0:
                        act(w("junk", at[0], at[0] + 16 * k), w("b%d" % i, t, 64 * k, 4), F.Identity, bias=1.0, scale=-1.0,
                            acc=w("acc", k, k + 1))
                        at[0] += 16 * k
                if pending and i > 1:
                    close(pending.pop(0))
                if k == 3:
                    scan(w("ph", 1, C), w("bb", 0, C - 1), w("aa", 0, C - 1), -320.0, A.mult, A.max)
                if k == 1:
                    scan(w("no", 1, C), w("sa", 0, C - 1), w("ones", 0, C - 1), 2.0, A.add, A.add)
                if k == 0:
                    tt(w("cd"), w("aa"), w("ph"), A.subtract)
            pending.append(i)
            if r == 0 and i == 1:
                for b in range(4):
                    quant(w("qe", 128 * b, 128 * b + 128), w("se", 128 * b, 128 * b + 128), w("eb", 3 - b, 515 - b))
                unpack(qx, sx)
            if i == 1:
                if r == 0:
                    act(w("sa"), ps(1, C), F.Sign, bias=-TINY)
                act(w("bb"), ps(2, C), F.Sign, bias=TINY, scale=-1.0)
                act(w("aa", 0, C - 1), w("sa", 0, C - 1), F.Identity, bias=-160.0, scale=480.0)
        for k in ON_SCALAR:
            act(w("acc", k, k + 1), w("acr", k, k + 1), F.Identity, bias=16.0 * k, scale=-1.0)
        if r == 0:
            late_constants()
        close(pending.pop(0))
        scan(w("no", C + 1, 2 * C), w("cd", 0, C - 1), w("no", 0, C - 1), 0.0, A.max, A.min)
        for b in range(4):
            act(plane("th", b), ps(4 + b, C), scale=0.5)
        unpack(w("ql%d" % r), w("sl%d" % r))
        if far:
            eno = to_list("eno", w("no"), 2 * C)
            ec = to_list("ec", ps(3, C), C)
            ts(w("nou"), eno, DOWN, A.add, 0.5, A.mult)
            tt(w("yy"), ec, w("acc"), A.add)
            ts(w("rk"), w("yy"), DOWN1, A.add)
        else:
            tt(w("mx"), w("bb"), w("aa"), A.max)
            ec = to_list("ec", ps(3, C), C)
            eno = to_list("eno", w("no"), 2 * C)
            tt(w("yy"), ec, w("acc"), A.add)
            ts(w("nou"), eno, DOWN, A.add, 0.5, A.mult)
            ts(w("rk"), w("yy"), DOWN1, A.add)
            scan(w("cs"), w("mx"), w("ni"), 1.0, A.min, A.max)
        W0, T1, WW, M1, PA, D0, D1, SO = [w("sm", K * j, K * j + K) for j in range(8)]
        early = [] if far else [0, 1][:r + 1]
        for b in early:
            act(plane("tp", b), ps(4 + b, C), scale=0.5)
        scatter(w("oo", 0, C), w("rk"), w("iota", 0, C))
        act(w("g1", 0, H), ind(w("oo", 0, C), w("nou", 0, 8)))
        if far:
            cp(w("g1", H, 2 * H), ind(w("oo", 0, C), w("nou", K, K + 8)))
        else:
            ecd = to_list("ecd", w("cd"), C)
            act(w("g1", H, 2 * H), ind(w("oo", 0, C), w("nou", K, K + 8)))
        act(w("oo", C, C + 1), w("oo", 0, 1))
        act(w("g2", R, 2 * R), ind(w("oo", 0, C), w("nou", K + 8, 2 * K)))
        act(w("g2", 0, R), ind(w("oo", 0, C + 1), w("nou", 8, K)))
        if not far:
            ts(T1, w("nioff"), w("cs", C - 1, C), A.is_equal, 1920.0, A.mult)
            ts(W0, ecd, -2.0, A.mult, UPW, A.add)
            tt(WW, W0, T1, A.subtract)
            tt(M1, WW, w("eno", C + 15, 2 * C, 16), A.max)
        e1 = to_list("e1", w("g1"), 2 * H)
        if not far:
            ts(D0, WW, 2.0, A.mult, UPX, A.add)
        ts(w("ao%d" % r), e1, DOWNC, A.add)
        send_lists(r)
        if far:
            tt(w("mx"), w("bb"), w("aa"), A.max)
            ecd = to_list("ecd", w("cd"), C)
            scan(w("cs"), w("mx"), w("ni"), 1.0, A.min, A.max)
            ts(W0, ecd, -2.0, A.mult, UPW, A.add)
            ts(T1, w("nioff"), w("cs", C - 1, C), A.is_equal, 1920.0, A.mult)
            e2 = to_list("e2", w("g2"), 2 * R)
            tt(WW, W0, T1, A.subtract)
            ts(w("ab2"), e2, DOWNC, A.add)
            tt(M1, WW, w("eno", C + 15, 2 * C, 16), A.max)
            ts(D0, WW, 2.0, A.mult, UPX, A.add)
        tt(PA, M1, w("eno", 15, C, 16), A.min)
        tt(D1, D0, w("dum"), A.min)
        late = [b for b in range(4) if b not in early]
        act(plane("tp", late[0]), ps(4 + late[0], C), scale=0.5)

        def own_mean(b):
            tt(w("z2", b, 4 * R, 4), ind(plane("th", b), w("ab2", 10, 20)), plane("gt", b, H, C), A.add)

        def own_picks():
            for b in range(4):
                act(plane("gt", b, H, C), ind(plane("th", b), w("ab2", 0, 10)))
            for b in late[1:]:
                act(plane("tp", b), ps(4 + b, C), scale=0.5)

        if far:
            own_picks()
            own_mean(0)
            tt(SO, PA, D1, A.max)
            own_mean(1)
            ts(w("sou"), SO, DOWN, A.add, 0.5, A.mult)
            own_mean(2)
            scatter(w("ll"), w("sou"), w("iota", 0, C))
            own_mean(3)
            tt(w("ll", 0, 1), w("ll", 0, 1), w("ll", C, C + 1), A.max)
        else:
            e2 = to_list("e2", w("g2"), 2 * R)
            tt(SO, PA, D1, A.max)
            ts(w("ab2"), e2, DOWNC, A.add)
            ts(w("sou"), SO, DOWN, A.add, 0.5, A.mult)
            scatter(w("ll"), w("sou"), w("iota", 0, C))
            own_picks()
            own_mean(0)
            tt(w("ll", 0, 1), w("ll", 0, 1), w("ll", C, C + 1), A.max)
            for b in range(1, 4):
                own_mean(b)
        act(w("lw"), ind(w("ll", 0, C), w("rk")))

        def own_products():
            quant(w("q2"), w("s2"), w("z2"))
            for k in range(4):
                mm(ps(4 + k, R), *part("qw", "sw", k), w("q2"), w("s2"))

        def own_layer():
            for k in range(4):
                act(plane("vv", k, H, C), ps(4 + k, R), scale=0.03125)

        if far:
            own_products()
            own_layer()
        al = "al%d" % r
        for b in range(4):
            act(plane("gt", b, 0, H), ind(plane("tp", b), w(al, 0, 8)))
            tt(w("z1", b, 4 * H, 4), ind(plane("tp", b), w(al, 8, 16)), plane("gt", b, 0, H), A.add)
            if b == 0 and not far:
                own_products()
        el = to_list("el", w("lw"), C)
        quant(w("q1"), w("s1"), w("z1"))
        for k in (0, 3, 1, 2):
            mm(ps(k, H), *part("qw", "sw", k), w("q1"), w("s1"))
        if not far:
            own_layer()
        ts(w("lu"), el, DOWNC, A.add)
        ts(plane("vv", 0, 0, H), ps(0, H), 0.03125, A.mult)
        for k in (3, 1, 2):
            act(plane("vv", k, 0, H), ps(k, H), scale=0.03125)
        act(plane("vg", 3), ind(plane("vv", 3), w("lu")))
        for lo, hi in HALVES:
            act(plane("vg", 2, lo, hi), ind(plane("vv", 2), w("lu", lo // 16, hi // 16)))
        for b in range(2):
            tt(w(XN, b, 4 * C, 4), ind(plane("vv", b), w("lu")), w(X, b, 4 * C, 4), A.add)
        tt(w(XN, 3, 4 * C, 4), plane("vg", 3), w(X, 3, 4 * C, 4), A.add)
        for lo, hi in HALVES:
            tt(w(XN, 4 * lo + 2, 4 * hi, 4), plane("vg", 2, lo, hi), w(X, 4 * lo + 2, 4 * hi, 4), A.add)
        if r == 2:
            act(w("lf"), w("lw"), F.Identity, bias=MID)
            dma("y", ext("lb"), (T.lf[0:128:16, :], [("lf", 0, C, 1)]))

    for j, (a, b) in enumerate(HALVES):
        quant(w("qx3", a, b), w("sx3", a, b), w("x3", 4 * a, 4 * b))
        mm(ps(j, b - a), w("qv"), w("sv"), w("qx3", a, b), w("sx3", a, b))
    (a, b), (c, d) = HALVES
    act(w("yb", a, b), ps(0, b - a))
    dma("s", (T.y[:, a:b], []), w("yb", a, b))
    cp(w("yb", c, d), ps(1, d - c))
    dma("y", ext("oc"), u8(w("qx3")))
    for k in range(4):
        dma("s" if k < 3 else "y", (T.osc[4 * k:4 * k + 4, :], []), (T.sx3[32 * k:32 * k + 4, :], [("sx3", 0, C, 1)]))
    dma("y", (T.y[:, c:d], []), w("yb", c, d))
    for s, n in total.items():
        wait("g", (s, n), {})
